import numpy as np
import ml_dtypes


def mxq(x, axis, fmt="e4m3"):
    dtype, down = {"e4m3": (ml_dtypes.float8_e4m3fn, 7), "e5m2": (ml_dtypes.float8_e5m2, 14)}[fmt]
    v = np.moveaxis(np.asarray(x, np.float32).astype(ml_dtypes.bfloat16).astype(np.float64), axis, -1)
    blocks = v.reshape(v.shape[:-1] + (-1, 32))
    amax = np.abs(blocks).max(-1, keepdims=True)
    byte = np.maximum(np.where(amax > 0, np.frexp(amax)[1] - 1 + 127, 0) - down, 1)
    scale = np.exp2(byte - 127.0)
    codes = (blocks / scale).astype(np.float32).astype(dtype).astype(np.float64)
    return np.moveaxis((codes * scale).reshape(v.shape), -1, axis)


WIDE = False


def mx_kscale(k):
    if not WIDE:
        return np.ones(k)
    levels = np.array([10, -10, 5, -5, 0])
    if k % 512:
        return np.exp2(np.random.permutation(np.resize(levels, k // 32))).repeat(32)
    a = np.empty((k // 512, 16))
    for p in range(k // 512):
        a[p, :8] = np.random.permutation(np.resize(levels, 8))
        for g in range(8):
            far = levels[np.abs(levels - a[p, g]) >= 10]
            a[p, g + 8] = far[np.random.randint(len(far))]
    return np.exp2(a.ravel()).repeat(32)


BF16 = ml_dtypes.bfloat16


def bf(x):
    return np.asarray(x, np.float32).astype(BF16)


def f64(x):
    return np.asarray(x).astype(np.float64)


E2M1 = np.array([0.0, 0.5, 1.0, 1.5, 2.0, 3.0, 4.0, 6.0, -0.0, -0.5, -1.0, -1.5, -2.0, -3.0, -4.0, -6.0])


def pack_weight(w, fmt):
    k, n = w.shape
    w = f64(bf(w)).reshape(k // 32, 32, n)
    amax = np.abs(w).max(1)
    if fmt == "e4m3":
        byte = np.frexp(amax)[1] - 1 + 127 - 7
    else:
        mant, ex = np.frexp(amax / 6.0)
        byte = np.where(mant > 0.5, ex, ex - 1) + 127
    byte = np.clip(np.where(amax > 0, byte, 1), 1, 254)
    scaled = (w * np.exp2(127.0 - byte)[:, None, :]).reshape(k, n).astype(np.float32)
    by_word = np.ascontiguousarray(scaled.reshape(k // 512, 128, 4, n).transpose(0, 1, 3, 2))
    if fmt == "e4m3":
        words = by_word.astype(ml_dtypes.float8_e4m3fn).view(np.uint8)
    else:
        c = by_word.astype(ml_dtypes.float4_e2m1fn).view(np.uint8) & 0xF
        words = c[..., 0::2] | (c[..., 1::2] << 4)
    return np.ascontiguousarray(words), np.ascontiguousarray(byte.astype(np.uint8).reshape(k // 512, 16, n))


def unpack_weight(words, scales, fmt):
    g, p, n, _ = words.shape
    if fmt == "e4m3":
        vals = np.ascontiguousarray(words).view(ml_dtypes.float8_e4m3fn).astype(np.float64)
    else:
        nib = np.empty((g, p, n, 4), np.uint8)
        nib[..., 0::2] = words & 0xF
        nib[..., 1::2] = words >> 4
        vals = E2M1[nib]
    vals = vals * np.repeat(np.exp2(scales.astype(np.float64) - 127.0), 8, axis=1)[..., None]
    return vals.transpose(0, 1, 3, 2).reshape(g * 512, n)
def pack4(w):
    words, scales = pack_weight(w, "e2m1")
    return words.reshape(words.shape[0], 128, -1), scales


def unpack4(words, scales):
    return unpack_weight(words.reshape(words.shape[0], 128, -1, 2), scales, "e2m1")


def planes(Y):
    n, m = Y.shape
    b = f64(bf(Y)).reshape(n // 32, 32, m)
    amax = np.abs(b).max(1)
    byte = np.clip(np.where(amax > 0, np.frexp(amax)[1] - 1 + 127 - 7, 1), 1, 254)
    codes = (b * np.exp2(127.0 - byte)[:, None, :]).reshape(n, m).astype(np.float32).astype(ml_dtypes.float8_e4m3fn).view(np.uint8)
    words = codes.reshape(n // 512, 128, 4, m).transpose(0, 1, 3, 2)
    return np.ascontiguousarray(words), np.ascontiguousarray(byte.astype(np.uint8).reshape(n // 512, 16, m))


R, M, K, RANK = 512, 2048, 1024, 4

BETA = 0.9
SPREAD = 0.6
NOISE = 0.5
PAST = 1.6

def rank_sum(u, v):
    return (u[:, None, :] * v[None, :, :]).sum(-1)

def share(rho, v):
    low = rank_sum(np.random.randn(M, RANK), v) / np.sqrt(RANK)
    return rho * (low + NOISE * np.random.randn(M, K)) / np.sqrt(K)

def setup_inputs():
    s = mx_kscale(K)
    rho = np.exp(SPREAD * np.random.randn(M, 1))
    v = np.random.randn(K, RANK)
    ga, gb, gc = share(rho, v), share(rho, v), share(rho, v)
    total = ga + gb + gc
    past = PAST * rho * np.random.randn(M, RANK) / np.sqrt(RANK)
    left = BETA * rank_sum(past[:R], past)
    trace = BETA * (past ** 2).sum() + (total ** 2).sum()
    x_words, x_scales = pack_weight((total[:R] * s).T, "e4m3")
    a_words, a_scales = pack4((ga / s).T)
    b_words, b_scales = pack_weight((gb / s).T, "e4m3")
    return {"x_words": x_words, "x_scales": x_scales, "a_words": a_words, "a_scales": a_scales,
            "b_words": b_words, "b_scales": b_scales, "c": bf((gc / s).T),
            "left": bf(left), "trace_scale": bf(np.full((1,), M / trace))}

def reference(x_words, x_scales, a_words, a_scales, b_words, b_scales, c, left, trace_scale):
    x = unpack_weight(x_words, x_scales, "e4m3")
    pa = x.T @ unpack4(a_words, a_scales)
    pb = x.T @ unpack_weight(b_words, b_scales, "e4m3")
    pc = x.T @ mxq(f64(c), 0, "e4m3")
    y = (f64(left) + pa + pb + pc) * f64(trace_scale)
    words, scales = planes(y.T)
    return y, words, scales

@@ -1,0 +1,325 @@
+from contextlib import ExitStack
+
+import concourse.mybir as mybir
+from concourse.masks import make_identity
+
+R, M, K = 512, 2048, 1024
+FLOPS = 3 * 2 * R * M * K
+
+F32 = mybir.dt.float32
+BF16 = mybir.dt.bfloat16
+I32 = mybir.dt.int32
+U32 = mybir.dt.uint32
+U8 = mybir.dt.uint8
+FP8X4 = mybir.dt.float8_e4m3fn_x4
+FP4X4 = mybir.dt.float4_e2m1fn_x4
+ALU = mybir.AluOpType
+ACT = mybir.ActivationFunctionType
+
+P = 128
+PACK = 4
+N = 512
+PASSES = K // (P * PACK)
+ROW_TILES = R // P
+GROUPS = M // N
+B_ROW = 4
+VECTOR_COLS = (336, 232, 232, 232)
+
+
+def tile_shampoo_left_statistics_k3_kernel(
+    tc, x_words, x_scales, a_words, a_scales, b_words, b_scales, c, left, trace_scale, out_0, out_1, out_2
+):
+    nc = tc.nc
+    with ExitStack() as ctx:
+        keep = ctx.enter_context(tc.tile_pool(name="keep", bufs=1))
+        stage = ctx.enter_context(tc.tile_pool(name="stage", bufs=3))
+        acc_pool = ctx.enter_context(tc.psum_pool(name="acc", bufs=6))
+        turn_pool = ctx.enter_context(tc.psum_pool(name="turn", bufs=2))
+        ctx.enter_context(tc.manual_schedule())
+
+        x_plane = keep.tile([P, PASSES, R], U8, align_bytes=64)
+        a_plane = keep.tile([P, PASSES, M], U8, align_bytes=64)
+        b_plane = keep.tile([P, PASSES, M], U8, align_bytes=64)
+        for plane in (x_plane, a_plane, b_plane):
+            nc.vector.memset(plane[:].bitcast(I32), 0)
+
+        scale_bf = keep.tile([P, 1], BF16)
+        nc.gpsimd.dma_start(out=scale_bf[:], in_=trace_scale.partition_broadcast(P))
+        scale = keep.tile([P, 1], F32)
+        nc.scalar.copy(out=scale[:], in_=scale_bf[:])
+        ident = keep.tile([P, P], F32)
+        make_identity(nc, ident[:])
+
+        def load_plane(plane, rows, first_row):
+            for q in range(4):
+                nc.sync.dma_start(
+                    out=plane[32 * q + first_row : 32 * q + first_row + 4, :, :].bitcast(I32),
+                    in_=rows[:, 4 * q : 4 * q + 4, :].rearrange("g r n -> r g n").bitcast(I32),
+                )
+
+        x_codes, a_codes, b_codes, c_raw, left_raw = {}, {}, {}, {}, {}
+
+        def load_x(g):
+            x_codes[g] = keep.tile([P, R], U32, name="x_codes%d" % g, align_bytes=64)
+            nc.sync.dma_start(
+                out=x_codes[g][:].bitcast(I32), in_=x_words[g].rearrange("p n t -> p (n t)").bitcast(I32)
+            )
+
+        def load_a(j):
+            a_codes[j] = keep.tile([P, PASSES, 2 * N], U8, name="a_codes%d" % j, align_bytes=64)
+            nc.sync.dma_start(
+                out=a_codes[j][:].bitcast(I32),
+                in_=a_words[:, :, 2 * N * j : 2 * N * (j + 1)].rearrange("g p b -> p g b").bitcast(I32),
+            )
+
+        def load_b(j):
+            b_codes[j] = keep.tile([P, PASSES, N], U32, name="b_codes%d" % j, align_bytes=64)
+            nc.sync.dma_start(
+                out=b_codes[j][:].bitcast(I32),
+                in_=b_words[:, :, N * j : N * (j + 1), :].rearrange("g p n t -> p g (n t)").bitcast(I32),
+            )
+
+        def load_c(j):
+            for g in range(PASSES):
+                c_raw[j, g] = keep.tile([P, PACK, N], BF16, name="c_raw%d_%d" % (j, g), align_bytes=64)
+                rows = c[P * PACK * g : P * PACK * (g + 1), N * j : N * (j + 1)]
+                nc.sync.dma_start(out=c_raw[j, g][:], in_=rows.rearrange("(p t) n -> p t n", t=PACK))
+
+        def load_left(j):
+            left_raw[j] = keep.tile([P, ROW_TILES, N], BF16, name="left_raw%d" % j, align_bytes=64)
+            nc.sync.dma_start(
+                out=left_raw[j][:], in_=left[:, N * j : N * (j + 1)].rearrange("(i p) n -> p i n", p=P)
+            )
+
+        load_plane(x_plane, x_scales, 0)
+        load_x(0)
+        load_a(0)
+        load_plane(a_plane, a_scales, 0)
+        load_x(1)
+        load_plane(b_plane, b_scales, B_ROW)
+        load_b(0)
+        load_c(0)
+        load_left(0)
+        for j in range(1, GROUPS):
+            load_a(j)
+            load_b(j)
+            load_c(j)
+            load_left(j)
+
+        c_grouped, c_codes, c_plane, left_scaled, acc, y, y_pairs, turned, y_grouped = ({} for each in range(9))
+        y_codes = {}
+        y_planes = keep.tile([P, R], U8, align_bytes=64)
+
+        def interleave_c(j, g):
+            grouped = stage.tile([P, N, PACK], BF16, name="c_grouped", align_bytes=64)
+            c_grouped[j, g] = grouped
+            split = VECTOR_COLS[j]
+            raw = c_raw[j, g]
+            nc.scalar.copy(
+                out=grouped[:, split:, :].rearrange("p (c i) t -> p c t i", i=4),
+                in_=raw[:, :, split:].rearrange("p t (c i) -> p c t i", i=4),
+            )
+            nc.vector.tensor_copy(
+                out=grouped[:, :split, :].rearrange("p (c i) t -> p c t i", i=4),
+                in_=raw[:, :, :split].rearrange("p t (c i) -> p c t i", i=4),
+            )
+
+        def quantize_c(j, g):
+            c_codes[j, g] = keep.tile([P, N], U32, name="c_codes%d_%d" % (j, g), align_bytes=64)
+            c_plane[j, g] = keep.tile([P, N], U8, name="c_plane%d_%d" % (j, g), align_bytes=64)
+            nc.vector.quantize_mx(
+                out=c_codes[j, g][:].bitcast(FP8X4),
+                scales=c_plane[j, g][:],
+                in_=c_grouped[j, g][:].rearrange("p n t -> p (n t)"),
+            )
+
+        def prepare_c(j):
+            for g in range(PASSES):
+                interleave_c(j, g)
+            for g in range(PASSES):
+                quantize_c(j, g)
+
+        def scale_left(j):
+            left_scaled[j] = stage.tile([P, ROW_TILES, N], F32, name="left_scaled", bufs=2)
+            if j == 0:
+                for i in range(ROW_TILES):
+                    nc.scalar.activation(
+                        out=left_scaled[j][:, i, :], in_=left_raw[j][:, i, :], func=ACT.Copy, scale=scale[:]
+                    )
+            else:
+                nc.vector.tensor_scalar(
+                    out=left_scaled[j][:], in0=left_raw[j][:], scalar1=scale[:], scalar2=None, op0=ALU.mult
+                )
+
+        def multiply(operand, n, g):
+            j, i = divmod(n, ROW_TILES)
+            if operand == "a" and g == 0:
+                acc[n] = acc_pool.tile([P, N], F32, name="acc")
+            cols = slice(N * j, N * (j + 1))
+            if operand == "a":
+                rhs, rhs_scale = a_codes[j][:, g, :].bitcast(FP4X4), a_plane[:, g, cols]
+            elif operand == "b":
+                rhs, rhs_scale = b_codes[j][:, g, :].bitcast(FP8X4), b_plane[B_ROW:, g, cols]
+            else:
+                rhs, rhs_scale = c_codes[j, g][:].bitcast(FP8X4), c_plane[j, g][:]
+            rows = slice(P * i, P * (i + 1))
+            nc.tensor.matmul_mx(
+                out=acc[n][:],
+                lhsT=x_codes[g][:, rows].bitcast(FP8X4),
+                lhsT_scale=x_plane[:, g, rows],
+                rhs=rhs,
+                rhs_scale=rhs_scale,
+                start=(operand == "a" and g == 0),
+                stop=(operand == "c" and g == PASSES - 1),
+            )
+
+        def multiply_given(n):
+            for operand in ("a", "b"):
+                for g in range(PASSES):
+                    multiply(operand, n, g)
+
+        def multiply_c(n):
+            for g in range(PASSES):
+                multiply("c", n, g)
+
+        def finish(n):
+            j, i = divmod(n, ROW_TILES)
+            y[n] = keep.tile([P, N], F32, name="y%d" % n)
+            nc.vector.scalar_tensor_tensor(
+                out=y[n][:], in0=acc[n][:], scalar=scale[:], in1=left_scaled[j][:, i, :], op0=ALU.mult, op1=ALU.add
+            )
+
+        def store_y(n):
+            j, i = divmod(n, ROW_TILES)
+            nc.sync.dma_start(out=out_0[P * i : P * (i + 1), N * j : N * (j + 1)], in_=y[n][:])
+
+        def round_y(n, on_vector=False):
+            y_pairs[n] = keep.tile([P, N], BF16, name="y_pairs%d" % n)
+            dst = y_pairs[n][:].rearrange("q (u c p e) -> q c u p e", u=2, p=4, e=2)
+            src = y[n][:].rearrange("q (c p u e) -> q c u p e", u=2, p=4, e=2)
+            if on_vector:
+                nc.vector.tensor_copy(out=dst, in_=src)
+            else:
+                nc.scalar.copy(out=dst, in_=src)
+
+        def turn(tiles):
+            bank = turn_pool.tile([P, len(tiles), 2, P], F32, name="turned")
+            turned[tiles] = bank
+            for s, n in enumerate(tiles):
+                words = y_pairs[n][:].bitcast(F32)
+                for u in range(2):
+                    nc.tensor.transpose(bank[:, s, u, :], words[:, P * u : P * (u + 1)], ident[:])
+
+        def gather(tiles):
+            grouped = stage.tile([P, len(tiles), P, 2], F32, name="y_grouped", align_bytes=64)
+            y_grouped[tiles] = grouped
+            nc.scalar.copy(out=grouped[:], in_=turned[tiles][:].rearrange("p s u i -> p s i u"))
+
+        def quantize_y(tiles):
+            j, i = divmod(tiles[0], ROW_TILES)
+            if i == 0:
+                y_codes[j] = keep.tile([P, R], U32, name="y_codes%d" % j, align_bytes=64)
+            cols = slice(P * i, P * (i + len(tiles)))
+            nc.vector.quantize_mx(
+                out=y_codes[j][:, cols].bitcast(FP8X4),
+                scales=y_planes[4 * j :, cols],
+                in_=y_grouped[tiles][:].rearrange("p s i u -> p (s i u)").bitcast(BF16),
+            )
+
+        def store_codes(j, cols):
+            nc.sync.dma_start(
+                out=out_1[j, :, cols, :].rearrange("p m t -> p (m t)").bitcast(I32),
+                in_=y_codes[j][:, cols].bitcast(I32),
+            )
+
+        def close(n):
+            multiply_c(n)
+            finish(n)
+            store_y(n)
+
+        def whole(n):
+            multiply_given(n)
+            close(n)
+
+        def pairs(j):
+            return (4 * j, 4 * j + 1), (4 * j + 2, 4 * j + 3)
+
+        def turn_group(j):
+            for tiles in pairs(j):
+                turn(tiles)
+            for tiles in pairs(j):
+                gather(tiles)
+
+        def planes_group(j):
+            for tiles in pairs(j):
+                quantize_y(tiles)
+            store_codes(j, slice(0, R))
+
+        for g in range(PASSES):
+            interleave_c(0, g)
+            quantize_c(0, g)
+        scale_left(0)
+        for operand in ("a", "b", "c"):
+            for g in range(PASSES):
+                for n in range(4):
+                    multiply(operand, n, g)
+        for n in range(4):
+            finish(n)
+            store_y(n)
+
+        prepare_c(1)
+        scale_left(1)
+        for n in range(4):
+            round_y(n)
+        for n in range(4, 8):
+            multiply_given(n)
+        for n in range(4, 8):
+            close(n)
+
+        prepare_c(2)
+        scale_left(2)
+        turn_group(0)
+        for n in range(4, 8):
+            round_y(n)
+        multiply_given(8)
+        multiply_given(9)
+        close(8)
+        planes_group(0)
+        close(9)
+        prepare_c(3)
+        whole(10)
+        scale_left(3)
+        turn_group(1)
+        whole(11)
+        for n in range(8, 12):
+            round_y(n)
+        planes_group(1)
+        whole(12)
+        round_y(12)
+        whole(13)
+        turn_group(2)
+        round_y(13)
+        whole(14)
+        round_y(14)
+        planes_group(2)
+        multiply_given(15)
+        multiply_c(15)
+        finish(15)
+        round_y(15, on_vector=True)
+        store_y(15)
+        turn((12, 13))
+        turn((14,))
+        gather((12, 13))
+        gather((14,))
+        turn((15,))
+        quantize_y((12, 13))
+        quantize_y((14,))
+        gather((15,))
+        store_codes(3, slice(0, 3 * P))
+        quantize_y((15,))
+        store_codes(3, slice(3 * P, R))
+        for q in range(4):
+            nc.sync.dma_start(
+                out=out_2[:, 4 * q : 4 * q + 4, :].bitcast(I32),
+                in_=y_planes[32 * q : 32 * q + 16, :].bitcast(I32),
+            )

@@ -23,7 +23,8 @@ PASSES = K // (P * PACK)
 ROW_TILES = R // P
 GROUPS = M // N
 B_ROW = 4
-VECTOR_COLS = (336, 232, 232, 232)
+VECTOR_COLS = {0: (336, 336), 1: (304, 208), 2: (304, 208), 3: (304, 208)}
+STORE_UNITS = ((0, 1, 2, 3), (4, 5, 6, 7), (8, 9), (10, 11), (12, 13), (14,), (15,))
 
 
 def tile_shampoo_left_statistics_k3_kernel(
@@ -38,24 +39,30 @@ def tile_shampoo_left_statistics_k3_kernel(
         ctx.enter_context(tc.manual_schedule())
 
         x_plane = keep.tile([P, PASSES, R], U8, align_bytes=64)
-        a_plane = keep.tile([P, PASSES, M], U8, align_bytes=64)
+        a_plane_first = keep.tile([P, PASSES, N], U8, align_bytes=64)
         b_plane = keep.tile([P, PASSES, M], U8, align_bytes=64)
-        for plane in (x_plane, a_plane, b_plane):
+        a_plane_rest = keep.tile([P, PASSES, M - N], U8, align_bytes=64)
+        for plane in (x_plane, a_plane_first, b_plane, a_plane_rest):
             nc.vector.memset(plane[:].bitcast(I32), 0)
-
-        scale_bf = keep.tile([P, 1], BF16)
-        nc.gpsimd.dma_start(out=scale_bf[:], in_=trace_scale.partition_broadcast(P))
+        scale_row = keep.tile([P, 2], BF16)
+        nc.vector.memset(scale_row[:], 0.0)
+        ones = keep.tile([P, P], BF16)
+        nc.vector.memset(ones[:], 1.0)
         scale = keep.tile([P, 1], F32)
-        nc.scalar.copy(out=scale[:], in_=scale_bf[:])
         ident = keep.tile([P, P], F32)
         make_identity(nc, ident[:])
 
-        def load_plane(plane, rows, first_row):
-            for q in range(4):
-                nc.sync.dma_start(
-                    out=plane[32 * q + first_row : 32 * q + first_row + 4, :, :].bitcast(I32),
-                    in_=rows[:, 4 * q : 4 * q + 4, :].rearrange("g r n -> r g n").bitcast(I32),
+        def load_plane(queue, plane, rows, first_row):
+            by_row = rows.rearrange("g (q r) n -> r q g n", r=4)
+            for r in range(4):
+                queue.dma_start(
+                    out=plane[first_row + r : P : 32, :, :].bitcast(I32), in_=by_row[r].bitcast(I32)
                 )
+
+        def spread_scale():
+            spread = turn_pool.tile([P, 2], F32, name="turned")
+            nc.tensor.matmul(spread[:], lhsT=ones[:], rhs=scale_row[:], start=True, stop=True)
+            nc.scalar.copy(out=scale[:], in_=spread[:, 0:1])
 
         x_codes, a_codes, b_codes, c_raw, left_raw = {}, {}, {}, {}, {}
 
@@ -79,11 +86,10 @@ def tile_shampoo_left_statistics_k3_kernel(
                 in_=b_words[:, :, N * j : N * (j + 1), :].rearrange("g p n t -> p g (n t)").bitcast(I32),
             )
 
-        def load_c(j):
-            for g in range(PASSES):
-                c_raw[j, g] = keep.tile([P, PACK, N], BF16, name="c_raw%d_%d" % (j, g), align_bytes=64)
-                rows = c[P * PACK * g : P * PACK * (g + 1), N * j : N * (j + 1)]
-                nc.sync.dma_start(out=c_raw[j, g][:], in_=rows.rearrange("(p t) n -> p t n", t=PACK))
+        def load_c(j, g):
+            c_raw[j, g] = keep.tile([P, PACK, N], BF16, name="c_raw%d_%d" % (j, g), align_bytes=64)
+            rows = c[P * PACK * g : P * PACK * (g + 1), N * j : N * (j + 1)]
+            nc.sync.dma_start(out=c_raw[j, g][:], in_=rows.rearrange("(p t) n -> p t n", t=PACK))
 
         def load_left(j):
             left_raw[j] = keep.tile([P, ROW_TILES, N], BF16, name="left_raw%d" % j, align_bytes=64)
@@ -91,19 +97,23 @@ def tile_shampoo_left_statistics_k3_kernel(
                 out=left_raw[j][:], in_=left[:, N * j : N * (j + 1)].rearrange("(i p) n -> p i n", p=P)
             )
 
-        load_plane(x_plane, x_scales, 0)
+        load_plane(nc.gpsimd, b_plane, b_scales, B_ROW)
+        load_plane(nc.gpsimd, a_plane_rest, a_scales[:, :, N:], 0)
+        load_plane(nc.sync, x_plane, x_scales, 0)
         load_x(0)
         load_a(0)
-        load_plane(a_plane, a_scales, 0)
+        load_plane(nc.sync, a_plane_first, a_scales[:, :, :N], 0)
         load_x(1)
-        load_plane(b_plane, b_scales, B_ROW)
+        nc.sync.dma_start(out=scale_row[0:1, 0:1], in_=trace_scale.partition_broadcast(1))
         load_b(0)
-        load_c(0)
+        load_c(0, 0)
+        load_c(0, 1)
         load_left(0)
         for j in range(1, GROUPS):
+            load_c(j, 0)
             load_a(j)
             load_b(j)
-            load_c(j)
+            load_c(j, 1)
             load_left(j)
 
         c_grouped, c_codes, c_plane, left_scaled, acc, y, y_pairs, turned, y_grouped = ({} for each in range(9))
@@ -113,7 +123,7 @@ def tile_shampoo_left_statistics_k3_kernel(
         def interleave_c(j, g):
             grouped = stage.tile([P, N, PACK], BF16, name="c_grouped", align_bytes=64)
             c_grouped[j, g] = grouped
-            split = VECTOR_COLS[j]
+            split = VECTOR_COLS[j][g]
             raw = c_raw[j, g]
             nc.scalar.copy(
                 out=grouped[:, split:, :].rearrange("p (c i) t -> p c t i", i=4),
@@ -133,22 +143,23 @@ def tile_shampoo_left_statistics_k3_kernel(
                 in_=c_grouped[j, g][:].rearrange("p n t -> p (n t)"),
             )
 
-        def prepare_c(j):
-            for g in range(PASSES):
-                interleave_c(j, g)
-            for g in range(PASSES):
-                quantize_c(j, g)
-
         def scale_left(j):
-            left_scaled[j] = stage.tile([P, ROW_TILES, N], F32, name="left_scaled", bufs=2)
+            left_scaled[j] = stage.tile([P, ROW_TILES * N], F32, name="left_scaled", bufs=2)
             if j == 0:
                 for i in range(ROW_TILES):
                     nc.scalar.activation(
-                        out=left_scaled[j][:, i, :], in_=left_raw[j][:, i, :], func=ACT.Copy, scale=scale[:]
+                        out=left_scaled[j][:, N * i : N * (i + 1)],
+                        in_=left_raw[j][:, i, :],
+                        func=ACT.Copy,
+                        scale=scale[:],
                     )
             else:
                 nc.vector.tensor_scalar(
-                    out=left_scaled[j][:], in0=left_raw[j][:], scalar1=scale[:], scalar2=None, op0=ALU.mult
+                    out=left_scaled[j][:],
+                    in0=left_raw[j][:].rearrange("p i n -> p (i n)"),
+                    scalar1=scale[:],
+                    scalar2=None,
+                    op0=ALU.mult,
                 )
 
         def multiply(operand, n, g):
@@ -157,7 +168,8 @@ def tile_shampoo_left_statistics_k3_kernel(
                 acc[n] = acc_pool.tile([P, N], F32, name="acc")
             cols = slice(N * j, N * (j + 1))
             if operand == "a":
-                rhs, rhs_scale = a_codes[j][:, g, :].bitcast(FP4X4), a_plane[:, g, cols]
+                rhs = a_codes[j][:, g, :].bitcast(FP4X4)
+                rhs_scale = a_plane_first[:, g, :] if j == 0 else a_plane_rest[:, g, N * (j - 1) : N * j]
             elif operand == "b":
                 rhs, rhs_scale = b_codes[j][:, g, :].bitcast(FP8X4), b_plane[B_ROW:, g, cols]
             else:
@@ -182,25 +194,47 @@ def tile_shampoo_left_statistics_k3_kernel(
             for g in range(PASSES):
                 multiply("c", n, g)
 
+        y_unit = {}
+
         def finish(n):
             j, i = divmod(n, ROW_TILES)
-            y[n] = keep.tile([P, N], F32, name="y%d" % n)
+            unit = [u for u in STORE_UNITS if n in u][0]
+            if n == unit[0]:
+                y_unit[unit] = keep.tile([P, len(unit) * N], F32, name="y%d" % n)
+            y[n] = y_unit[unit][:, N * (n - unit[0]) : N * (n - unit[0] + 1)]
             nc.vector.scalar_tensor_tensor(
-                out=y[n][:], in0=acc[n][:], scalar=scale[:], in1=left_scaled[j][:, i, :], op0=ALU.mult, op1=ALU.add
+                out=y[n],
+                in0=acc[n][:],
+                scalar=scale[:],
+                in1=left_scaled[j][:, N * i : N * (i + 1)],
+                op0=ALU.mult,
+                op1=ALU.add,
+            )
+            if n == unit[-1]:
+                first = unit[0] % ROW_TILES
+                rows = out_0[P * first : P * (first + len(unit)), N * j : N * (j + 1)]
+                nc.sync.dma_start(
+                    out=rows.rearrange("(i p) n -> p i n", p=P),
+                    in_=y_unit[unit][:].rearrange("p (i n) -> p i n", n=N),
+                )
+
+        def round_y(n):
+            y_pairs[n] = keep.tile([P, N], BF16, name="y_pairs%d" % n)
+            nc.scalar.copy(
+                out=y_pairs[n][:].rearrange("q (u c p e) -> q c u p e", u=2, p=4, e=2),
+                in_=y[n].rearrange("q (c p u e) -> q c u p e", u=2, p=4, e=2),
             )
 
-        def store_y(n):
+        def round_from_bank(n):
             j, i = divmod(n, ROW_TILES)
-            nc.sync.dma_start(out=out_0[P * i : P * (i + 1), N * j : N * (j + 1)], in_=y[n][:])
-
-        def round_y(n, on_vector=False):
             y_pairs[n] = keep.tile([P, N], BF16, name="y_pairs%d" % n)
-            dst = y_pairs[n][:].rearrange("q (u c p e) -> q c u p e", u=2, p=4, e=2)
-            src = y[n][:].rearrange("q (c p u e) -> q c u p e", u=2, p=4, e=2)
-            if on_vector:
-                nc.vector.tensor_copy(out=dst, in_=src)
-            else:
-                nc.scalar.copy(out=dst, in_=src)
+            dst = y_pairs[n][:].rearrange("q (u p e) -> q u p e", u=2, e=2)
+            sums = acc[n][:].rearrange("q (p u e) -> q u p e", u=2, e=2)
+            added = left_scaled[j][:, N * i : N * (i + 1)].rearrange("q (p u e) -> q u p e", u=2, e=2)
+            for u in range(2):
+                nc.vector.scalar_tensor_tensor(
+                    out=dst[:, u], in0=sums[:, u], scalar=scale[:], in1=added[:, u], op0=ALU.mult, op1=ALU.add
+                )
 
         def turn(tiles):
             bank = turn_pool.tile([P, len(tiles), 2, P], F32, name="turned")
@@ -235,7 +269,6 @@ def tile_shampoo_left_statistics_k3_kernel(
         def close(n):
             multiply_c(n)
             finish(n)
-            store_y(n)
 
         def whole(n):
             multiply_given(n)
@@ -258,25 +291,34 @@ def tile_shampoo_left_statistics_k3_kernel(
         for g in range(PASSES):
             interleave_c(0, g)
             quantize_c(0, g)
-        scale_left(0)
         for operand in ("a", "b", "c"):
             for g in range(PASSES):
                 for n in range(4):
                     multiply(operand, n, g)
-        for n in range(4):
-            finish(n)
-            store_y(n)
-
-        prepare_c(1)
+            if operand == "a":
+                spread_scale()
+        scale_left(0)
+        interleave_c(1, 0)
+        finish(0)
+        quantize_c(1, 0)
+        finish(1)
+        interleave_c(1, 1)
+        finish(2)
+        finish(3)
+        quantize_c(1, 1)
         scale_left(1)
         for n in range(4):
             round_y(n)
         for n in range(4, 8):
             multiply_given(n)
-        for n in range(4, 8):
-            close(n)
-
-        prepare_c(2)
+        interleave_c(2, 0)
+        close(4)
+        close(5)
+        quantize_c(2, 0)
+        interleave_c(2, 1)
+        close(6)
+        close(7)
+        quantize_c(2, 1)
         scale_left(2)
         turn_group(0)
         for n in range(4, 8):
@@ -284,10 +326,13 @@ def tile_shampoo_left_statistics_k3_kernel(
         multiply_given(8)
         multiply_given(9)
         close(8)
-        planes_group(0)
+        interleave_c(3, 0)
         close(9)
-        prepare_c(3)
+        planes_group(0)
+        quantize_c(3, 0)
+        interleave_c(3, 1)
         whole(10)
+        quantize_c(3, 1)
         scale_left(3)
         turn_group(1)
         whole(11)
@@ -304,9 +349,8 @@ def tile_shampoo_left_statistics_k3_kernel(
         planes_group(2)
         multiply_given(15)
         multiply_c(15)
+        round_from_bank(15)
         finish(15)
-        round_y(15, on_vector=True)
-        store_y(15)
         turn((12, 13))
         turn((14,))
         gather((12, 13))
@@ -319,7 +363,8 @@ def tile_shampoo_left_statistics_k3_kernel(
         quantize_y((15,))
         store_codes(3, slice(3 * P, R))
         for q in range(4):
-            nc.sync.dma_start(
+            queue = nc.scalar if q % 2 == 0 else nc.sync
+            queue.dma_start(
                 out=out_2[:, 4 * q : 4 * q + 4, :].bitcast(I32),
                 in_=y_planes[32 * q : 32 * q + 16, :].bitcast(I32),
             )

@@ -23,7 +23,14 @@ PASSES = K // (P * PACK)
 ROW_TILES = R // P
 GROUPS = M // N
 B_ROW = 4
-VECTOR_COLS = {0: (336, 336), 1: (304, 208), 2: (304, 208), 3: (304, 208)}
+VECTOR_COLS = 304
+A_EARLY = 2 * N
+B_EARLY = N
+BANKS = 8
+LAG = 1
+FIRST_STEP = 1
+FIRST_TURN = 9
+TURN_EVERY = 2
 STORE_UNITS = ((0, 1, 2, 3), (4, 5, 6, 7), (8, 9), (10, 11), (12, 13), (14,), (15,))
 
 
@@ -34,15 +41,23 @@ def tile_shampoo_left_statistics_k3_kernel(
     with ExitStack() as ctx:
         keep = ctx.enter_context(tc.tile_pool(name="keep", bufs=1))
         stage = ctx.enter_context(tc.tile_pool(name="stage", bufs=3))
-        acc_pool = ctx.enter_context(tc.psum_pool(name="acc", bufs=6))
-        turn_pool = ctx.enter_context(tc.psum_pool(name="turn", bufs=2))
+        psum = ctx.enter_context(tc.psum_pool(name="psum", bufs=1))
         ctx.enter_context(tc.manual_schedule())
 
+        handed_out = []
+
+        def next_bank(shape):
+            bank = psum.tile(shape, F32, name="bank%d" % (len(handed_out) % BANKS))
+            handed_out.append(bank)
+            return bank
+
+
         x_plane = keep.tile([P, PASSES, R], U8, align_bytes=64)
-        a_plane_first = keep.tile([P, PASSES, N], U8, align_bytes=64)
-        b_plane = keep.tile([P, PASSES, M], U8, align_bytes=64)
-        a_plane_rest = keep.tile([P, PASSES, M - N], U8, align_bytes=64)
-        for plane in (x_plane, a_plane_first, b_plane, a_plane_rest):
+        a_early = keep.tile([P, PASSES, A_EARLY], U8, align_bytes=64)
+        b_early = keep.tile([P, PASSES, B_EARLY], U8, align_bytes=64)
+        b_late = keep.tile([P, PASSES, M - B_EARLY], U8, align_bytes=64)
+        a_late = keep.tile([P, PASSES, M - A_EARLY], U8, align_bytes=64)
+        for plane in (x_plane, a_early, b_early, b_late, a_late):
             nc.vector.memset(plane[:].bitcast(I32), 0)
         scale_row = keep.tile([P, 2], BF16)
         nc.vector.memset(scale_row[:], 0.0)
@@ -50,17 +65,17 @@ def tile_shampoo_left_statistics_k3_kernel(
         nc.vector.memset(ones[:], 1.0)
         scale = keep.tile([P, 1], F32)
         ident = keep.tile([P, P], F32)
-        make_identity(nc, ident[:])
+        nc.vector.memset(ident[:], 0.0)
 
-        def load_plane(queue, plane, rows, first_row):
+        def load_plane(queue, plane, rows, first_row, which):
             by_row = rows.rearrange("g (q r) n -> r q g n", r=4)
-            for r in range(4):
+            for r in which:
                 queue.dma_start(
                     out=plane[first_row + r : P : 32, :, :].bitcast(I32), in_=by_row[r].bitcast(I32)
                 )
 
         def spread_scale():
-            spread = turn_pool.tile([P, 2], F32, name="turned")
+            spread = psum.tile([P, 2], F32, name="bank%d" % (BANKS - 1))
             nc.tensor.matmul(spread[:], lhsT=ones[:], rhs=scale_row[:], start=True, stop=True)
             nc.scalar.copy(out=scale[:], in_=spread[:, 0:1])
 
@@ -97,24 +112,32 @@ def tile_shampoo_left_statistics_k3_kernel(
                 out=left_raw[j][:], in_=left[:, N * j : N * (j + 1)].rearrange("(i p) n -> p i n", p=P)
             )
 
-        load_plane(nc.gpsimd, b_plane, b_scales, B_ROW)
-        load_plane(nc.gpsimd, a_plane_rest, a_scales[:, :, N:], 0)
-        load_plane(nc.sync, x_plane, x_scales, 0)
+        load_plane(nc.gpsimd, b_late, b_scales[:, :, B_EARLY:], B_ROW, range(4))
+        make_identity(nc, ident[:], nomemset=True)
+        load_plane(nc.gpsimd, a_late, a_scales[:, :, A_EARLY:], 0, range(4))
+        load_plane(nc.sync, x_plane, x_scales, 0, range(4))
         load_x(0)
         load_a(0)
-        load_plane(nc.sync, a_plane_first, a_scales[:, :, :N], 0)
+        load_plane(nc.sync, a_early, a_scales[:, :, :A_EARLY], 0, range(4))
+        load_c(0, 0)
+        load_plane(nc.sync, b_early, b_scales[:, :, :B_EARLY], B_ROW, range(2))
         load_x(1)
+        load_plane(nc.sync, b_early, b_scales[:, :, :B_EARLY], B_ROW, range(2, 4))
         nc.sync.dma_start(out=scale_row[0:1, 0:1], in_=trace_scale.partition_broadcast(1))
         load_b(0)
-        load_c(0, 0)
         load_c(0, 1)
+        load_c(1, 0)
+        load_a(1)
+        load_b(1)
+        load_c(1, 1)
         load_left(0)
-        for j in range(1, GROUPS):
+        for j in range(2, GROUPS):
             load_c(j, 0)
+            load_left(j - 1)
+            load_c(j, 1)
             load_a(j)
             load_b(j)
-            load_c(j, 1)
-            load_left(j)
+        load_left(GROUPS - 1)
 
         c_grouped, c_codes, c_plane, left_scaled, acc, y, y_pairs, turned, y_grouped = ({} for each in range(9))
         y_codes = {}
@@ -123,7 +146,7 @@ def tile_shampoo_left_statistics_k3_kernel(
         def interleave_c(j, g):
             grouped = stage.tile([P, N, PACK], BF16, name="c_grouped", align_bytes=64)
             c_grouped[j, g] = grouped
-            split = VECTOR_COLS[j][g]
+            split = VECTOR_COLS
             raw = c_raw[j, g]
             nc.scalar.copy(
                 out=grouped[:, split:, :].rearrange("p (c i) t -> p c t i", i=4),
@@ -143,35 +166,34 @@ def tile_shampoo_left_statistics_k3_kernel(
                 in_=c_grouped[j, g][:].rearrange("p n t -> p (n t)"),
             )
 
-        def scale_left(j):
-            left_scaled[j] = stage.tile([P, ROW_TILES * N], F32, name="left_scaled", bufs=2)
+        def prepare_c(j):
+            for g in range(PASSES):
+                interleave_c(j, g)
+                quantize_c(j, g)
+
+        def scale_left(n):
+            j, i = divmod(n, ROW_TILES)
+            left_scaled[n] = stage.tile([P, N], F32, name="left_scaled")
             if j == 0:
-                for i in range(ROW_TILES):
-                    nc.scalar.activation(
-                        out=left_scaled[j][:, N * i : N * (i + 1)],
-                        in_=left_raw[j][:, i, :],
-                        func=ACT.Copy,
-                        scale=scale[:],
-                    )
+                nc.scalar.activation(out=left_scaled[n][:], in_=left_raw[j][:, i, :], func=ACT.Copy, scale=scale[:])
             else:
                 nc.vector.tensor_scalar(
-                    out=left_scaled[j][:],
-                    in0=left_raw[j][:].rearrange("p i n -> p (i n)"),
-                    scalar1=scale[:],
-                    scalar2=None,
-                    op0=ALU.mult,
+                    out=left_scaled[n][:], in0=left_raw[j][:, i, :], scalar1=scale[:], scalar2=None, op0=ALU.mult
                 )
+
+        def window(early, late, early_cols, first_row, j, g):
+            if N * j < early_cols:
+                return early[first_row:, g, N * j : N * (j + 1)]
+            return late[first_row:, g, N * j - early_cols : N * (j + 1) - early_cols]
 
         def multiply(operand, n, g):
             j, i = divmod(n, ROW_TILES)
             if operand == "a" and g == 0:
-                acc[n] = acc_pool.tile([P, N], F32, name="acc")
-            cols = slice(N * j, N * (j + 1))
+                acc[n] = next_bank([P, N])
             if operand == "a":
-                rhs = a_codes[j][:, g, :].bitcast(FP4X4)
-                rhs_scale = a_plane_first[:, g, :] if j == 0 else a_plane_rest[:, g, N * (j - 1) : N * j]
+                rhs, rhs_scale = a_codes[j][:, g, :].bitcast(FP4X4), window(a_early, a_late, A_EARLY, 0, j, g)
             elif operand == "b":
-                rhs, rhs_scale = b_codes[j][:, g, :].bitcast(FP8X4), b_plane[B_ROW:, g, cols]
+                rhs, rhs_scale = b_codes[j][:, g, :].bitcast(FP8X4), window(b_early, b_late, B_EARLY, B_ROW, j, g)
             else:
                 rhs, rhs_scale = c_codes[j, g][:].bitcast(FP8X4), c_plane[j, g][:]
             rows = slice(P * i, P * (i + 1))
@@ -197,7 +219,7 @@ def tile_shampoo_left_statistics_k3_kernel(
         y_unit = {}
 
         def finish(n):
-            j, i = divmod(n, ROW_TILES)
+            j = n // ROW_TILES
             unit = [u for u in STORE_UNITS if n in u][0]
             if n == unit[0]:
                 y_unit[unit] = keep.tile([P, len(unit) * N], F32, name="y%d" % n)
@@ -206,7 +228,7 @@ def tile_shampoo_left_statistics_k3_kernel(
                 out=y[n],
                 in0=acc[n][:],
                 scalar=scale[:],
-                in1=left_scaled[j][:, N * i : N * (i + 1)],
+                in1=left_scaled[n][:],
                 op0=ALU.mult,
                 op1=ALU.add,
             )
@@ -226,18 +248,17 @@ def tile_shampoo_left_statistics_k3_kernel(
             )
 
         def round_from_bank(n):
-            j, i = divmod(n, ROW_TILES)
             y_pairs[n] = keep.tile([P, N], BF16, name="y_pairs%d" % n)
             dst = y_pairs[n][:].rearrange("q (u p e) -> q u p e", u=2, e=2)
             sums = acc[n][:].rearrange("q (p u e) -> q u p e", u=2, e=2)
-            added = left_scaled[j][:, N * i : N * (i + 1)].rearrange("q (p u e) -> q u p e", u=2, e=2)
+            added = left_scaled[n][:].rearrange("q (p u e) -> q u p e", u=2, e=2)
             for u in range(2):
                 nc.vector.scalar_tensor_tensor(
                     out=dst[:, u], in0=sums[:, u], scalar=scale[:], in1=added[:, u], op0=ALU.mult, op1=ALU.add
                 )
 
         def turn(tiles):
-            bank = turn_pool.tile([P, len(tiles), 2, P], F32, name="turned")
+            bank = next_bank([P, len(tiles), 2, P])
             turned[tiles] = bank
             for s, n in enumerate(tiles):
                 words = y_pairs[n][:].bitcast(F32)
@@ -245,7 +266,7 @@ def tile_shampoo_left_statistics_k3_kernel(
                     nc.tensor.transpose(bank[:, s, u, :], words[:, P * u : P * (u + 1)], ident[:])
 
         def gather(tiles):
-            grouped = stage.tile([P, len(tiles), P, 2], F32, name="y_grouped", align_bytes=64)
+            grouped = stage.tile([P, len(tiles), P, 2], F32, name="y_grouped", align_bytes=64, bufs=4)
             y_grouped[tiles] = grouped
             nc.scalar.copy(out=grouped[:], in_=turned[tiles][:].rearrange("p s u i -> p s i u"))
 
@@ -266,14 +287,6 @@ def tile_shampoo_left_statistics_k3_kernel(
                 in_=y_codes[j][:, cols].bitcast(I32),
             )
 
-        def close(n):
-            multiply_c(n)
-            finish(n)
-
-        def whole(n):
-            multiply_given(n)
-            close(n)
-
         def pairs(j):
             return (4 * j, 4 * j + 1), (4 * j + 2, 4 * j + 3)
 
@@ -288,69 +301,46 @@ def tile_shampoo_left_statistics_k3_kernel(
                 quantize_y(tiles)
             store_codes(j, slice(0, R))
 
-        for g in range(PASSES):
-            interleave_c(0, g)
-            quantize_c(0, g)
+        prepare_c(0)
         for operand in ("a", "b", "c"):
             for g in range(PASSES):
-                for n in range(4):
+                for n in range(ROW_TILES):
                     multiply(operand, n, g)
             if operand == "a":
                 spread_scale()
+        prepare_c(1)
+        c_steps = [(step, j, g) for j in range(2, GROUPS) for g in range(PASSES) for step in (interleave_c, quantize_c)]
+        last = ROW_TILES * GROUPS - 1
+        opened = ROW_TILES
+        rounded = 0
         scale_left(0)
-        interleave_c(1, 0)
-        finish(0)
-        quantize_c(1, 0)
-        finish(1)
-        interleave_c(1, 1)
-        finish(2)
-        finish(3)
-        quantize_c(1, 1)
-        scale_left(1)
-        for n in range(4):
-            round_y(n)
-        for n in range(4, 8):
-            multiply_given(n)
-        interleave_c(2, 0)
-        close(4)
-        close(5)
-        quantize_c(2, 0)
-        interleave_c(2, 1)
-        close(6)
-        close(7)
-        quantize_c(2, 1)
-        scale_left(2)
-        turn_group(0)
-        for n in range(4, 8):
-            round_y(n)
-        multiply_given(8)
-        multiply_given(9)
-        close(8)
-        interleave_c(3, 0)
-        close(9)
-        planes_group(0)
-        quantize_c(3, 0)
-        interleave_c(3, 1)
-        whole(10)
-        quantize_c(3, 1)
-        scale_left(3)
-        turn_group(1)
-        whole(11)
-        for n in range(8, 12):
-            round_y(n)
-        planes_group(1)
-        whole(12)
-        round_y(12)
-        whole(13)
-        turn_group(2)
-        round_y(13)
-        whole(14)
-        round_y(14)
-        planes_group(2)
-        multiply_given(15)
-        multiply_c(15)
-        round_from_bank(15)
-        finish(15)
+        for n in range(last + 1):
+            j = n // ROW_TILES
+            if j > 0:
+                lead = GROUPS - 1 - j
+                for ahead in range(opened, min(n + lead, ROW_TILES * (j + 1) - 1) + 1):
+                    multiply_given(ahead)
+                    opened = ahead + 1
+                multiply_c(n)
+            if n == last:
+                round_from_bank(n)
+                finish(n)
+            else:
+                scale_left(n + LAG)
+                finish(n)
+                if 0 <= n - FIRST_STEP < len(c_steps):
+                    step, cj, cg = c_steps[n - FIRST_STEP]
+                    step(cj, cg)
+                lag = LAG if n < last - ROW_TILES else 0
+                for m in range(rounded, n - lag + 1):
+                    round_y(m)
+                    rounded = m + 1
+            for group in range(GROUPS - 1):
+                turn_at = FIRST_TURN + TURN_EVERY * group
+                if n == turn_at:
+                    turn_group(group)
+                if n == min(turn_at + TURN_EVERY, last - 1):
+                    planes_group(group)
         turn((12, 13))
         turn((14,))
         gather((12, 13))

@@ -177,8 +177,13 @@ def tile_shampoo_left_statistics_k3_kernel(
             if j == 0:
                 nc.scalar.activation(out=left_scaled[n][:], in_=left_raw[j][:, i, :], func=ACT.Copy, scale=scale[:])
             else:
-                nc.vector.tensor_scalar(
-                    out=left_scaled[n][:], in0=left_raw[j][:, i, :], scalar1=scale[:], scalar2=None, op0=ALU.mult
+                nc.gpsimd.tensor_scalar(
+                    out=left_scaled[n][:],
+                    in0=left_raw[j][:, i, :],
+                    scalar1=scale[:],
+                    scalar2=0.0,
+                    op0=ALU.mult,
+                    op1=ALU.add,
                 )
 
         def window(early, late, early_cols, first_row, j, g):

from contextlib import ExitStack

import concourse.mybir as mybir
from concourse.masks import make_identity

R, M, K = 512, 2048, 1024
FLOPS = 3 * 2 * R * M * K

F32 = mybir.dt.float32
BF16 = mybir.dt.bfloat16
I32 = mybir.dt.int32
U32 = mybir.dt.uint32
U8 = mybir.dt.uint8
FP8X4 = mybir.dt.float8_e4m3fn_x4
FP4X4 = mybir.dt.float4_e2m1fn_x4
ALU = mybir.AluOpType
ACT = mybir.ActivationFunctionType

P = 128
PACK = 4
N = 512
PASSES = K // (P * PACK)
ROW_TILES = R // P
GROUPS = M // N
B_ROW = 4
VECTOR_COLS = 304
A_EARLY = 2 * N
B_EARLY = N
BANKS = 8
LAG = 1
FIRST_STEP = 1
FIRST_TURN = 9
TURN_EVERY = 2
STORE_UNITS = ((0, 1, 2, 3), (4, 5, 6, 7), (8, 9), (10, 11), (12, 13), (14,), (15,))


def tile_shampoo_left_statistics_k3_kernel(
    tc, x_words, x_scales, a_words, a_scales, b_words, b_scales, c, left, trace_scale, out_0, out_1, out_2
):
    nc = tc.nc
    with ExitStack() as ctx:
        keep = ctx.enter_context(tc.tile_pool(name="keep", bufs=1))
        stage = ctx.enter_context(tc.tile_pool(name="stage", bufs=3))
        psum = ctx.enter_context(tc.psum_pool(name="psum", bufs=1))
        ctx.enter_context(tc.manual_schedule())

        handed_out = []

        def next_bank(shape):
            bank = psum.tile(shape, F32, name="bank%d" % (len(handed_out) % BANKS))
            handed_out.append(bank)
            return bank


        x_plane = keep.tile([P, PASSES, R], U8, align_bytes=64)
        a_early = keep.tile([P, PASSES, A_EARLY], U8, align_bytes=64)
        b_early = keep.tile([P, PASSES, B_EARLY], U8, align_bytes=64)
        b_late = keep.tile([P, PASSES, M - B_EARLY], U8, align_bytes=64)
        a_late = keep.tile([P, PASSES, M - A_EARLY], U8, align_bytes=64)
        for plane in (x_plane, a_early, b_early, b_late, a_late):
            nc.vector.memset(plane[:].bitcast(I32), 0)
        scale_row = keep.tile([P, 2], BF16)
        nc.vector.memset(scale_row[:], 0.0)
        ones = keep.tile([P, P], BF16)
        nc.vector.memset(ones[:], 1.0)
        scale = keep.tile([P, 1], F32)
        ident = keep.tile([P, P], F32)
        nc.vector.memset(ident[:], 0.0)

        def load_plane(queue, plane, rows, first_row, which):
            by_row = rows.rearrange("g (q r) n -> r q g n", r=4)
            for r in which:
                queue.dma_start(
                    out=plane[first_row + r : P : 32, :, :].bitcast(I32), in_=by_row[r].bitcast(I32)
                )

        def spread_scale():
            spread = psum.tile([P, 2], F32, name="bank%d" % (BANKS - 1))
            nc.tensor.matmul(spread[:], lhsT=ones[:], rhs=scale_row[:], start=True, stop=True)
            nc.scalar.copy(out=scale[:], in_=spread[:, 0:1])

        x_codes, a_codes, b_codes, c_raw, left_raw = {}, {}, {}, {}, {}

        def load_x(g):
            x_codes[g] = keep.tile([P, R], U32, name="x_codes%d" % g, align_bytes=64)
            nc.sync.dma_start(
                out=x_codes[g][:].bitcast(I32), in_=x_words[g].rearrange("p n t -> p (n t)").bitcast(I32)
            )

        def load_a(j):
            a_codes[j] = keep.tile([P, PASSES, 2 * N], U8, name="a_codes%d" % j, align_bytes=64)
            nc.sync.dma_start(
                out=a_codes[j][:].bitcast(I32),
                in_=a_words[:, :, 2 * N * j : 2 * N * (j + 1)].rearrange("g p b -> p g b").bitcast(I32),
            )

        def load_b(j):
            b_codes[j] = keep.tile([P, PASSES, N], U32, name="b_codes%d" % j, align_bytes=64)
            nc.sync.dma_start(
                out=b_codes[j][:].bitcast(I32),
                in_=b_words[:, :, N * j : N * (j + 1), :].rearrange("g p n t -> p g (n t)").bitcast(I32),
            )

        def load_c(j, g):
            c_raw[j, g] = keep.tile([P, PACK, N], BF16, name="c_raw%d_%d" % (j, g), align_bytes=64)
            rows = c[P * PACK * g : P * PACK * (g + 1), N * j : N * (j + 1)]
            nc.sync.dma_start(out=c_raw[j, g][:], in_=rows.rearrange("(p t) n -> p t n", t=PACK))

        def load_left(j):
            left_raw[j] = keep.tile([P, ROW_TILES, N], BF16, name="left_raw%d" % j, align_bytes=64)
            nc.sync.dma_start(
                out=left_raw[j][:], in_=left[:, N * j : N * (j + 1)].rearrange("(i p) n -> p i n", p=P)
            )

        load_plane(nc.gpsimd, b_late, b_scales[:, :, B_EARLY:], B_ROW, range(4))
        make_identity(nc, ident[:], nomemset=True)
        load_plane(nc.gpsimd, a_late, a_scales[:, :, A_EARLY:], 0, range(4))
        load_plane(nc.sync, x_plane, x_scales, 0, range(4))
        load_x(0)
        load_a(0)
        load_plane(nc.sync, a_early, a_scales[:, :, :A_EARLY], 0, range(4))
        load_c(0, 0)
        load_plane(nc.sync, b_early, b_scales[:, :, :B_EARLY], B_ROW, range(2))
        load_x(1)
        load_plane(nc.sync, b_early, b_scales[:, :, :B_EARLY], B_ROW, range(2, 4))
        nc.sync.dma_start(out=scale_row[0:1, 0:1], in_=trace_scale.partition_broadcast(1))
        load_b(0)
        load_c(0, 1)
        load_c(1, 0)
        load_a(1)
        load_b(1)
        load_c(1, 1)
        load_left(0)
        for j in range(2, GROUPS):
            load_c(j, 0)
            load_left(j - 1)
            load_c(j, 1)
            load_a(j)
            load_b(j)
        load_left(GROUPS - 1)

        c_grouped, c_codes, c_plane, left_scaled, acc, y, y_pairs, turned, y_grouped = ({} for each in range(9))
        y_codes = {}
        y_planes = keep.tile([P, R], U8, align_bytes=64)

        def interleave_c(j, g):
            grouped = stage.tile([P, N, PACK], BF16, name="c_grouped", align_bytes=64)
            c_grouped[j, g] = grouped
            split = VECTOR_COLS
            raw = c_raw[j, g]
            nc.scalar.copy(
                out=grouped[:, split:, :].rearrange("p (c i) t -> p c t i", i=4),
                in_=raw[:, :, split:].rearrange("p t (c i) -> p c t i", i=4),
            )
            nc.vector.tensor_copy(
                out=grouped[:, :split, :].rearrange("p (c i) t -> p c t i", i=4),
                in_=raw[:, :, :split].rearrange("p t (c i) -> p c t i", i=4),
            )

        def quantize_c(j, g):
            c_codes[j, g] = keep.tile([P, N], U32, name="c_codes%d_%d" % (j, g), align_bytes=64)
            c_plane[j, g] = keep.tile([P, N], U8, name="c_plane%d_%d" % (j, g), align_bytes=64)
            nc.vector.quantize_mx(
                out=c_codes[j, g][:].bitcast(FP8X4),
                scales=c_plane[j, g][:],
                in_=c_grouped[j, g][:].rearrange("p n t -> p (n t)"),
            )

        def prepare_c(j):
            for g in range(PASSES):
                interleave_c(j, g)
                quantize_c(j, g)

        def scale_left(n):
            j, i = divmod(n, ROW_TILES)
            left_scaled[n] = stage.tile([P, N], F32, name="left_scaled")
            if j == 0:
                nc.scalar.activation(out=left_scaled[n][:], in_=left_raw[j][:, i, :], func=ACT.Copy, scale=scale[:])
            else:
                nc.gpsimd.tensor_scalar(
                    out=left_scaled[n][:],
                    in0=left_raw[j][:, i, :],
                    scalar1=scale[:],
                    scalar2=0.0,
                    op0=ALU.mult,
                    op1=ALU.add,
                )

        def window(early, late, early_cols, first_row, j, g):
            if N * j < early_cols:
                return early[first_row:, g, N * j : N * (j + 1)]
            return late[first_row:, g, N * j - early_cols : N * (j + 1) - early_cols]

        def multiply(operand, n, g):
            j, i = divmod(n, ROW_TILES)
            if operand == "a" and g == 0:
                acc[n] = next_bank([P, N])
            if operand == "a":
                rhs, rhs_scale = a_codes[j][:, g, :].bitcast(FP4X4), window(a_early, a_late, A_EARLY, 0, j, g)
            elif operand == "b":
                rhs, rhs_scale = b_codes[j][:, g, :].bitcast(FP8X4), window(b_early, b_late, B_EARLY, B_ROW, j, g)
            else:
                rhs, rhs_scale = c_codes[j, g][:].bitcast(FP8X4), c_plane[j, g][:]
            rows = slice(P * i, P * (i + 1))
            nc.tensor.matmul_mx(
                out=acc[n][:],
                lhsT=x_codes[g][:, rows].bitcast(FP8X4),
                lhsT_scale=x_plane[:, g, rows],
                rhs=rhs,
                rhs_scale=rhs_scale,
                start=(operand == "a" and g == 0),
                stop=(operand == "c" and g == PASSES - 1),
            )

        def multiply_given(n):
            for operand in ("a", "b"):
                for g in range(PASSES):
                    multiply(operand, n, g)

        def multiply_c(n):
            for g in range(PASSES):
                multiply("c", n, g)

        y_unit = {}

        def finish(n):
            j = n // ROW_TILES
            unit = [u for u in STORE_UNITS if n in u][0]
            if n == unit[0]:
                y_unit[unit] = keep.tile([P, len(unit) * N], F32, name="y%d" % n)
            y[n] = y_unit[unit][:, N * (n - unit[0]) : N * (n - unit[0] + 1)]
            nc.vector.scalar_tensor_tensor(
                out=y[n],
                in0=acc[n][:],
                scalar=scale[:],
                in1=left_scaled[n][:],
                op0=ALU.mult,
                op1=ALU.add,
            )
            if n == unit[-1]:
                first = unit[0] % ROW_TILES
                rows = out_0[P * first : P * (first + len(unit)), N * j : N * (j + 1)]
                nc.sync.dma_start(
                    out=rows.rearrange("(i p) n -> p i n", p=P),
                    in_=y_unit[unit][:].rearrange("p (i n) -> p i n", n=N),
                )

        def round_y(n):
            y_pairs[n] = keep.tile([P, N], BF16, name="y_pairs%d" % n)
            nc.scalar.copy(
                out=y_pairs[n][:].rearrange("q (u c p e) -> q c u p e", u=2, p=4, e=2),
                in_=y[n].rearrange("q (c p u e) -> q c u p e", u=2, p=4, e=2),
            )

        def round_from_bank(n):
            y_pairs[n] = keep.tile([P, N], BF16, name="y_pairs%d" % n)
            dst = y_pairs[n][:].rearrange("q (u p e) -> q u p e", u=2, e=2)
            sums = acc[n][:].rearrange("q (p u e) -> q u p e", u=2, e=2)
            added = left_scaled[n][:].rearrange("q (p u e) -> q u p e", u=2, e=2)
            for u in range(2):
                nc.vector.scalar_tensor_tensor(
                    out=dst[:, u], in0=sums[:, u], scalar=scale[:], in1=added[:, u], op0=ALU.mult, op1=ALU.add
                )

        def turn(tiles):
            bank = next_bank([P, len(tiles), 2, P])
            turned[tiles] = bank
            for s, n in enumerate(tiles):
                words = y_pairs[n][:].bitcast(F32)
                for u in range(2):
                    nc.tensor.transpose(bank[:, s, u, :], words[:, P * u : P * (u + 1)], ident[:])

        def gather(tiles):
            grouped = stage.tile([P, len(tiles), P, 2], F32, name="y_grouped", align_bytes=64, bufs=4)
            y_grouped[tiles] = grouped
            nc.scalar.copy(out=grouped[:], in_=turned[tiles][:].rearrange("p s u i -> p s i u"))

        def quantize_y(tiles):
            j, i = divmod(tiles[0], ROW_TILES)
            if i == 0:
                y_codes[j] = keep.tile([P, R], U32, name="y_codes%d" % j, align_bytes=64)
            cols = slice(P * i, P * (i + len(tiles)))
            nc.vector.quantize_mx(
                out=y_codes[j][:, cols].bitcast(FP8X4),
                scales=y_planes[4 * j :, cols],
                in_=y_grouped[tiles][:].rearrange("p s i u -> p (s i u)").bitcast(BF16),
            )

        def store_codes(j, cols):
            nc.sync.dma_start(
                out=out_1[j, :, cols, :].rearrange("p m t -> p (m t)").bitcast(I32),
                in_=y_codes[j][:, cols].bitcast(I32),
            )

        def pairs(j):
            return (4 * j, 4 * j + 1), (4 * j + 2, 4 * j + 3)

        def turn_group(j):
            for tiles in pairs(j):
                turn(tiles)
            for tiles in pairs(j):
                gather(tiles)

        def planes_group(j):
            for tiles in pairs(j):
                quantize_y(tiles)
            store_codes(j, slice(0, R))

        prepare_c(0)
        for operand in ("a", "b", "c"):
            for g in range(PASSES):
                for n in range(ROW_TILES):
                    multiply(operand, n, g)
            if operand == "a":
                spread_scale()
        prepare_c(1)
        c_steps = [(step, j, g) for j in range(2, GROUPS) for g in range(PASSES) for step in (interleave_c, quantize_c)]
        last = ROW_TILES * GROUPS - 1
        opened = ROW_TILES
        rounded = 0
        scale_left(0)
        for n in range(last + 1):
            j = n // ROW_TILES
            if j > 0:
                lead = GROUPS - 1 - j
                for ahead in range(opened, min(n + lead, ROW_TILES * (j + 1) - 1) + 1):
                    multiply_given(ahead)
                    opened = ahead + 1
                multiply_c(n)
            if n == last:
                round_from_bank(n)
                finish(n)
            else:
                scale_left(n + LAG)
                finish(n)
                if 0 <= n - FIRST_STEP < len(c_steps):
                    step, cj, cg = c_steps[n - FIRST_STEP]
                    step(cj, cg)
                lag = LAG if n < last - ROW_TILES else 0
                for m in range(rounded, n - lag + 1):
                    round_y(m)
                    rounded = m + 1
            for group in range(GROUPS - 1):
                turn_at = FIRST_TURN + TURN_EVERY * group
                if n == turn_at:
                    turn_group(group)
                if n == min(turn_at + TURN_EVERY, last - 1):
                    planes_group(group)
        turn((12, 13))
        turn((14,))
        gather((12, 13))
        gather((14,))
        turn((15,))
        quantize_y((12, 13))
        quantize_y((14,))
        gather((15,))
        store_codes(3, slice(0, 3 * P))
        quantize_y((15,))
        store_codes(3, slice(3 * P, R))
        for q in range(4):
            queue = nc.scalar if q % 2 == 0 else nc.sync
            queue.dma_start(
                out=out_2[:, 4 * q : 4 * q + 4, :].bitcast(I32),
                in_=y_planes[32 * q : 32 * q + 16, :].bitcast(I32),
            )
